import numpy as np
import ml_dtypes


def mxq(x, axis, fmt="e4m3"):
    dtype, down = {"e4m3": (ml_dtypes.float8_e4m3fn, 7), "e5m2": (ml_dtypes.float8_e5m2, 14)}[fmt]
    v = np.moveaxis(np.asarray(x, np.float32).astype(ml_dtypes.bfloat16).astype(np.float64), axis, -1)
    blocks = v.reshape(v.shape[:-1] + (-1, 32))
    amax = np.abs(blocks).max(-1, keepdims=True)
    byte = np.maximum(np.where(amax > 0, np.frexp(amax)[1] - 1 + 127, 0) - down, 1)
    scale = np.exp2(byte - 127.0)
    codes = (blocks / scale).astype(np.float32).astype(dtype).astype(np.float64)
    return np.moveaxis((codes * scale).reshape(v.shape), -1, axis)


WIDE = False


def mx_kscale(k):
    if not WIDE:
        return np.ones(k)
    levels = np.array([10, -10, 5, -5, 0])
    if k % 512:
        return np.exp2(np.random.permutation(np.resize(levels, k // 32))).repeat(32)
    a = np.empty((k // 512, 16))
    for p in range(k // 512):
        a[p, :8] = np.random.permutation(np.resize(levels, 8))
        for g in range(8):
            far = levels[np.abs(levels - a[p, g]) >= 10]
            a[p, g + 8] = far[np.random.randint(len(far))]
    return np.exp2(a.ravel()).repeat(32)


def f64(x):
    return np.asarray(x).astype(np.float64)


def striped(idx):
    return np.tile(idx.reshape(-1, 16).T, (8, 1)).astype(np.uint16)


def unstriped(offs):
    return offs[:16].T.reshape(-1).astype(np.int64)


E2M1 = np.array([0.0, 0.5, 1.0, 1.5, 2.0, 3.0, 4.0, 6.0, -0.0, -0.5, -1.0, -1.5, -2.0, -3.0, -4.0, -6.0])


def pack_weight(w, fmt):
    k, n = w.shape
    w = f64(np.asarray(w, np.float32).astype(ml_dtypes.bfloat16)).reshape(k // 32, 32, n)
    amax = np.abs(w).max(1)
    if fmt == "e4m3":
        byte = np.frexp(amax)[1] - 1 + 127 - 7
    else:
        mant, ex = np.frexp(amax / 6.0)
        byte = np.where(mant > 0.5, ex, ex - 1) + 127
    byte = np.clip(np.where(amax > 0, byte, 1), 1, 254)
    scaled = (w * np.exp2(127.0 - byte)[:, None, :]).reshape(k, n).astype(np.float32)
    by_word = np.ascontiguousarray(scaled.reshape(k // 512, 128, 4, n).transpose(0, 1, 3, 2))
    if fmt == "e4m3":
        words = by_word.astype(ml_dtypes.float8_e4m3fn).view(np.uint8)
    else:
        c = by_word.astype(ml_dtypes.float4_e2m1fn).view(np.uint8) & 0xF
        words = (c[..., 0::2] | (c[..., 1::2] << 4)).reshape(k // 512, 128, 2 * n)
    return np.ascontiguousarray(words), np.ascontiguousarray(byte.astype(np.uint8).reshape(k // 512, 16, n))


def unpack_weight(words, scales, fmt):
    g, _, n = scales.shape
    words = np.ascontiguousarray(words).reshape(g, 128, n, -1)
    if fmt == "e4m3":
        vals = words.view(ml_dtypes.float8_e4m3fn).astype(np.float64)
    else:
        nib = np.empty((g, 128, n, 4), np.uint8)
        nib[..., 0::2] = words & 0xF
        nib[..., 1::2] = words >> 4
        vals = E2M1[nib]
    vals = vals * np.repeat(np.exp2(scales.astype(np.float64) - 127.0), 8, axis=1)[..., None]
    return vals.transpose(0, 1, 3, 2).reshape(g * 512, n)


def gelu(v):
    return 0.5 * v * (1.0 + np.tanh(np.sqrt(2.0 / np.pi) * (v + 0.044715 * v**3)))


K, T, S, H, S2, T3, T2, P = 1536, 2048, 512, 1024, 512, 2048, 1024, 512

def setup_inputs():
    n = np.random.standard_normal
    s = mx_kscale(K)[:, None]
    u = mx_kscale(H)[:, None]
    tab_words, tab_scales = pack_weight(n((K, T)) * s, "e4m3")
    tab2_words, tab2_scales = pack_weight(n((H, T3)) / np.sqrt(H) / u, "e4m3")
    return {
        "tab_words": tab_words, "tab_scales": tab_scales,
        "tab2_words": tab2_words, "tab2_scales": tab2_scales,
        "offs": striped(np.random.permutation(T)[:S]),
        "offs2": striped(np.random.permutation(T3)[:S2]),
        "offs3": striped(np.random.permutation(T2)[:S]),
        "pos1": striped(np.random.permutation(T2)[:P]),
        "pos2": striped(np.random.permutation(T2)[:P]),
        "w1": (1.3 * n((K, H)) / np.sqrt(K) / s).astype(np.float32),
        "gain": (np.exp(0.3 * n(H)) * u[:, 0]).astype(np.float32),
        "res": (0.6 * n((H, S)) * u).astype(np.float32),
        "wgs": np.exp(0.3 * n((128, S))).astype(np.float32),
        "page0": (n((H, T2)) * u).astype(np.float32),
        "gain2": np.exp(0.3 * n(H)).astype(np.float32),
        "rake": (0.7 * n((S2, P))).astype(np.float32),
        "flow": np.exp(0.3 * n(S2)).astype(np.float32),
    }

def reference(tab_words, tab_scales, tab2_words, tab2_scales, offs, offs2, offs3, pos1, pos2,
              w1, gain, res, wgs, page0, gain2, rake, flow):
    v = unpack_weight(tab_words, tab_scales, "e4m3")[:, unstriped(offs)]
    v2 = unpack_weight(tab2_words, tab2_scales, "e4m3")[:, unstriped(offs2)]
    h = f64(gain)[:, None] * np.tanh(mxq(f64(w1), 0, "e4m3").T @ v) + f64(res)
    page = f64(page0).copy()
    page[:, unstriped(offs3)] = np.tile(f64(wgs), (H // 128, 1)) * h
    x = mxq(f64(gain2)[:, None] * page, 0, "e4m3")
    e = v2.T @ x
    return np.maximum(e[:, unstriped(pos1)] + f64(rake), f64(flow)[:, None] * e[:, unstriped(pos2)])

@@ -1,0 +1,345 @@
+from contextlib import ExitStack
+
+import concourse.mybir as mybir
+from concourse.masks import make_identity
+
+K, T, S, H, S2, T3, T2, NOUT = 1536, 2048, 512, 1024, 512, 2048, 1024, 512
+FLOPS = 2 * K * H * S + 2 * H * S2 * T2
+
+F32 = mybir.dt.float32
+BF16 = mybir.dt.bfloat16
+I32 = mybir.dt.int32
+U32 = mybir.dt.uint32
+U16 = mybir.dt.uint16
+U8 = mybir.dt.uint8
+FP8X4 = mybir.dt.float8_e4m3fn_x4
+MULT = mybir.AluOpType.mult
+ADD = mybir.AluOpType.add
+MAX = mybir.AluOpType.max
+COPY = mybir.ActivationFunctionType.Copy
+TANH = mybir.ActivationFunctionType.Tanh
+
+P = 128
+PACK = 4
+PASS = P * PACK
+KP = K // PASS
+RP = H // PASS
+SLICES = RP * PACK
+HALF = T2 // 2
+MT = S2 // P
+KB = 1024
+
+
+def tile_list_thickener_reagent_scores_kernel(
+    tc, tab_words, tab_scales, tab2_words, tab2_scales, offs, offs2, offs3, pos1, pos2,
+    w1, gain, res, wgs, page0, gain2, rake, flow, out,
+):
+    nc = tc.nc
+    with ExitStack() as ctx:
+        held = ctx.enter_context(tc.tile_pool(name="held", bufs=1))
+        lay = ctx.enter_context(tc.tile_pool(name="lay", bufs=1))
+        ring = ctx.enter_context(tc.tile_pool(name="ring", bufs=2))
+        psum = ctx.enter_context(tc.psum_pool(name="psum", bufs=8))
+
+        def kept(shape, dtype, name):
+            return held.tile(shape, dtype, name=name, align_bytes=64)
+
+        def laid(shape, dtype, name, at):
+            return lay.tile(shape, dtype, name=name, align_bytes=64, offset=at)
+
+        def bank(name):
+            return psum.tile([P, PASS], F32, name=name, tag="bank")
+
+        lists = {}
+        for name in ("offs", "offs2", "offs3", "pos1", "pos2"):
+            lists[name] = held.tile([P, S // 16], U16, name="list_" + name)
+
+        tab_w = [laid([P, T], U32, "tab_w%d" % a, 8 * KB * a) for a in range(KP)]
+        w_raw = {}
+        for b in range(RP):
+            for a in range(KP):
+                w_raw[a, b] = laid([P, PACK, PASS], F32, "w_raw%d%d" % (a, b), (24 + 8 * (KP * b + a)) * KB)
+        tab2_w = [kept([P, T3], U32, "tab2_w%d" % b) for b in range(RP)]
+        tab_s = kept([P, T], U8, "tab_s")
+        tab2_s = kept([P, T3], U8, "tab2_s")
+        page = [kept([P, T2], F32, "page%d" % s) for s in range(SLICES)]
+        res_t = [kept([P, S], F32, "res%d" % s) for s in range(SLICES)]
+        rake_t = [kept([P, NOUT], F32, "rake%d" % m) for m in range(MT)]
+        wgs_raw = kept([P, S], F32, "wgs_raw")
+        gain_t = kept([P, RP, PACK], F32, "gain_t")
+        gain2_t = kept([P, RP, PACK], F32, "gain2_t")
+        flow_t = kept([P, MT], F32, "flow_t")
+        ident = kept([P, P], F32, "ident")
+
+        res_rows = res.rearrange("(b p t) j -> b t p j", b=RP, t=PACK)
+        page_rows = page0.rearrange("(b p t) n -> b t p n", b=RP, t=PACK)
+
+        def load_list(name, src):
+            nc.sync.dma_start(lists[name][:], src)
+
+        def load_words(dst, src):
+            nc.sync.dma_start(out=dst[:].bitcast(I32), in_=src.rearrange("p n t -> p (n t)").bitcast(I32))
+
+        def load_w(a, b):
+            rows = w1[a * PASS : (a + 1) * PASS, b * PASS : (b + 1) * PASS]
+            nc.sync.dma_start(out=w_raw[a, b][:], in_=rows.rearrange("(p j) c -> p j c", j=PACK))
+
+        def load_res(s):
+            nc.sync.dma_start(out=res_t[s][:], in_=res_rows[s // PACK, s % PACK])
+
+        def load_page(s):
+            nc.sync.dma_start(out=page[s][:], in_=page_rows[s // PACK, s % PACK])
+
+        def load_scales(queue, dst, src, passes):
+            for q in range(4):
+                queue.dma_start(
+                    out=dst[32 * q : 32 * q + 4 * passes, :].bitcast(I32),
+                    in_=src[:, 4 * q : 4 * q + 4, :].bitcast(I32),
+                )
+
+        nc.vector.memset(tab_s[:].bitcast(I32), 0)
+        load_scales(nc.scalar, tab_s, tab_scales, KP)
+        make_identity(nc, ident[:])
+        nc.vector.memset(tab2_s[:].bitcast(I32), 0)
+
+        load_words(tab_w[0], tab_words[0])
+        load_list("offs", offs)
+        load_w(0, 0)
+        nc.sync.dma_start(out=wgs_raw[:], in_=wgs)
+        load_w(1, 0)
+        load_words(tab_w[1], tab_words[1])
+        nc.sync.dma_start(out=gain_t[:], in_=gain.rearrange("(b p t) -> p b t", b=RP, t=PACK))
+        load_w(2, 0)
+        load_words(tab_w[2], tab_words[2])
+        load_list("offs3", offs3)
+        load_res(0)
+        load_res(1)
+        load_page(0)
+        load_w(0, 1)
+        nc.sync.dma_start(out=gain2_t[:], in_=gain2.rearrange("(b p t) -> p b t", b=RP, t=PACK))
+        load_res(2)
+        load_page(1)
+        load_w(1, 1)
+        load_res(3)
+        load_page(2)
+        load_w(2, 1)
+        load_res(4)
+        load_res(5)
+        load_page(4)
+        load_page(3)
+        load_res(6)
+        load_res(7)
+        load_page(5)
+        load_page(6)
+        load_page(7)
+        load_list("offs2", offs2)
+        load_scales(nc.sync, tab2_s, tab2_scales, RP)
+        for b in range(RP):
+            load_words(tab2_w[b], tab2_words[b])
+        load_list("pos1", pos1)
+        load_list("pos2", pos2)
+        with nc.allow_non_contiguous_dma(reason="one factor a partition"):
+            nc.sync.dma_start(out=flow_t[:], in_=flow.rearrange("(m p) -> p m", p=P))
+        for m in range(MT):
+            nc.sync.dma_start(out=rake_t[m][:], in_=rake[m * P : (m + 1) * P, :])
+
+        turned = bank("turned")
+        for c in range(4):
+            nc.tensor.transpose(turned[:, c * P : (c + 1) * P], wgs_raw[:, c * P : (c + 1) * P], ident[:])
+        spread = kept([P, PACK, 4, 4, 32], F32, "spread")
+        for rep in range(4):
+            nc.scalar.copy(out=spread[:, :, :, rep, :], in_=turned[:].rearrange("j (c q t) -> j t c q", c=4, t=PACK))
+        wgs_t = []
+        for t in range(PACK):
+            back = bank("back%d" % t)
+            for c in range(4):
+                nc.tensor.transpose(
+                    back[:, c * P : (c + 1) * P], spread[:, t, c].rearrange("j r q -> j (r q)"), ident[:]
+                )
+            if t < PACK - 1:
+                dealt = kept([P, S], F32, "wgs_t%d" % t)
+            else:
+                dealt = laid([P, S], F32, "wgs_t%d" % t, 72 * KB)
+            nc.scalar.copy(out=dealt[:], in_=back[:])
+            wgs_t.append(dealt)
+
+        v_w = [kept([P, S], U32, "v_w%d" % a) for a in range(KP)]
+        v_s = kept([P, S], U8, "v_s")
+        w_codes, w_scales = {}, {}
+
+        def gather_v(a):
+            nc.vector.tensor_copy(v_w[a][:], tab_w[a][:].indirect(lists["offs"][:]))
+
+        def quantise_w(a, b):
+            grouped = ring.tile([P, PACK, P, PACK], BF16, name="w_grouped", align_bytes=64)
+            dst = grouped[:].rearrange("p t m j -> p m j t")
+            src = w_raw[a, b][:].rearrange("p j (m t) -> p m j t", t=PACK)
+            if b == 0:
+                nc.vector.tensor_copy(out=dst, in_=src)
+            else:
+                nc.scalar.copy(out=dst, in_=src)
+            w_codes[a, b] = kept([P, PASS], U32, "w_codes%d%d" % (a, b))
+            w_scales[a, b] = kept([P, PASS], U8, "w_scales%d%d" % (a, b))
+            nc.vector.quantize_mx(
+                out=w_codes[a, b][:].bitcast(FP8X4), scales=w_scales[a, b][:],
+                in_=grouped[:].rearrange("p t m j -> p (t m j)"),
+            )
+
+        gather_v(0)
+        quantise_w(0, 0)
+        quantise_w(1, 0)
+        gather_v(1)
+        nc.vector.tensor_copy(v_s[:], tab_s[:].indirect(lists["offs"][:]))
+        quantise_w(2, 0)
+        gather_v(2)
+
+        squashed, feature = {}, {}
+
+        def first_product(s):
+            b, t = divmod(s, PACK)
+            z = bank("z%d" % s)
+            cols = slice(t * P, (t + 1) * P)
+            for a in range(KP):
+                nc.tensor.matmul_mx(
+                    out=z[:], lhsT=w_codes[a, b][:, cols].bitcast(FP8X4), lhsT_scale=w_scales[a, b][:, cols],
+                    rhs=v_w[a][:].bitcast(FP8X4), rhs_scale=v_s[4 * a : P, :],
+                    start=(a == 0), stop=(a == KP - 1),
+                )
+            squashed[s] = ring.tile([P, S], F32, name="squashed", bufs=4)
+            nc.scalar.activation(out=squashed[s][:], in_=z[:], func=TANH)
+
+        def make_feature(s):
+            b, t = divmod(s, PACK)
+            if s < SLICES - 1:
+                feature[s] = ring.tile([P, S], F32, name="feature", bufs=3)
+            else:
+                feature[s] = laid([P, S], F32, "feature_last", 74 * KB)
+            nc.vector.scalar_tensor_tensor(
+                out=feature[s][:], in0=squashed[s][:], scalar=gain_t[:, b, t : t + 1], in1=res_t[s][:],
+                op0=MULT, op1=ADD,
+            )
+
+        def scatter(s):
+            nc.vector.tensor_tensor(
+                page[s][:].indirect(lists["offs3"][:]), feature[s][:], wgs_t[s % PACK][:], MULT
+            )
+
+        pairs = {}
+        for h in range(2):
+            pairs[0, h] = laid([P, 2, HALF, 2], BF16, "pairs0%d" % h, (64 + 4 * h) * KB)
+            pairs[1, h] = laid([P, 2, HALF, 2], BF16, "pairs1%d" % h, (24 + 4 * h) * KB)
+        x_grouped = {
+            (0, 0): laid([P, HALF, PACK], BF16, "x_grouped00", 0),
+            (0, 1): laid([P, HALF, PACK], BF16, "x_grouped01", 4 * KB),
+            (1, 0): laid([P, HALF, PACK], BF16, "x_grouped10", 12 * KB),
+            (1, 1): laid([P, HALF, PACK], BF16, "x_grouped11", 76 * KB),
+        }
+        x_codes = [laid([P, T2], U32, "x_codes0", 8 * KB), laid([P, T2], U32, "x_codes1", 16 * KB)]
+        x_scales = [laid([P, T2], U8, "x_scales0", 75 * KB), laid([P, T2], U8, "x_scales1", 20 * KB)]
+
+        def round_page(s, h):
+            b, t = divmod(s, PACK)
+            nc.scalar.activation(
+                out=pairs[b, h][:, t // 2, :, t % 2], in_=page[s][:, h * HALF : (h + 1) * HALF],
+                func=COPY, scale=gain2_t[:, b, t : t + 1],
+            )
+
+        def weave_x(b, h):
+            nc.scalar.copy(
+                out=x_grouped[b, h][:].bitcast(U32),
+                in_=pairs[b, h][:].bitcast(U32).rearrange("p u n one -> p n (u one)"),
+            )
+
+        def quantise_x(b, h):
+            cols = slice(h * HALF, (h + 1) * HALF)
+            nc.vector.quantize_mx(
+                out=x_codes[b][:, cols].bitcast(FP8X4), scales=x_scales[b][:, cols],
+                in_=x_grouped[b, h][:].rearrange("p n t -> p (n t)"),
+            )
+
+        for s in range(PACK):
+            first_product(s)
+        make_feature(0)
+        for s in range(PACK - 1):
+            make_feature(s + 1)
+            scatter(s)
+            quantise_w(s, 1)
+        for s in range(PACK, SLICES):
+            first_product(s)
+        for s in range(PACK - 1, SLICES):
+            if s + 1 < SLICES:
+                make_feature(s + 1)
+            scatter(s)
+        for s in range(SLICES - 1):
+            for h in range(2):
+                round_page(s, h)
+            if s == PACK - 1:
+                for h in range(2):
+                    weave_x(0, h)
+        for h in range(2):
+            round_page(SLICES - 1, h)
+            weave_x(1, h)
+
+        v2_w, v2_s = {}, {}
+
+        def gather_v2(g, words_at, scales_at):
+            part = lists["offs2"][:, g * 16 : (g + 1) * 16]
+            v2_s[g] = laid([P, S2 // 2], U8, "v2_s%d" % g, scales_at)
+            nc.vector.tensor_copy(v2_s[g][:], tab2_s[:].indirect(part))
+            for b in range(RP):
+                v2_w[b, g] = laid([P, S2 // 2], U32, "v2_w%d%d" % (b, g), words_at + b * KB)
+                nc.vector.tensor_copy(v2_w[b, g][:], tab2_w[b][:].indirect(part))
+
+        for h in range(2):
+            quantise_x(0, h)
+        gather_v2(0, 72 * KB, 74 * KB)
+        for h in range(2):
+            quantise_x(1, h)
+        gather_v2(1, 76 * KB, 78 * KB)
+
+        scores = []
+        for m in range(MT):
+            g, mm = divmod(m, 2)
+            cols = slice(mm * P, (mm + 1) * P)
+            e = kept([P, T2], F32, "scores%d" % m)
+            for h in range(2):
+                ncols = slice(h * HALF, (h + 1) * HALF)
+                acc = bank("acc%d%d" % (m, h))
+                for b in range(RP):
+                    nc.tensor.matmul_mx(
+                        out=acc[:], lhsT=v2_w[b, g][:, cols].bitcast(FP8X4), lhsT_scale=v2_s[g][4 * b : P, cols],
+                        rhs=x_codes[b][:, ncols].bitcast(FP8X4), rhs_scale=x_scales[b][:, ncols],
+                        start=(b == 0), stop=(b == RP - 1),
+                    )
+                nc.scalar.copy(out=e[:, ncols], in_=acc[:])
+            scores.append(e)
+
+        pieces = [(m, 0, NOUT) for m in range(MT - 1)] + [(MT - 1, 0, NOUT // 2), (MT - 1, NOUT // 2, NOUT)]
+        left, right = {}, {}
+
+        def fetch_left(i):
+            m, lo, hi = pieces[i]
+            left[i] = laid([P, hi - lo], F32, "left%d" % i, (32 + 2 * (i % 2)) * KB)
+            nc.vector.tensor_tensor(
+                left[i][:], scores[m][:].indirect(lists["pos1"][:, lo // 16 : hi // 16]), rake_t[m][:, lo:hi], ADD
+            )
+
+        def fetch_right(i):
+            m, lo, hi = pieces[i]
+            right[i] = laid([P, hi - lo], F32, "right%d" % i, (36 + 2 * (i % 2)) * KB)
+            nc.vector.tensor_copy(right[i][:], scores[m][:].indirect(lists["pos2"][:, lo // 16 : hi // 16]))
+
+        def finish(i):
+            m, lo, hi = pieces[i]
+            result = laid([P, hi - lo], F32, "result%d" % i, (40 + 2 * (i % 3)) * KB)
+            nc.vector.scalar_tensor_tensor(
+                out=result[:], in0=right[i][:], scalar=flow_t[:, m : m + 1], in1=left[i][:], op0=MULT, op1=MAX
+            )
+            nc.sync.dma_start(out=out[m * P : (m + 1) * P, lo:hi], in_=result[:])
+
+        for i in range(len(pieces)):
+            fetch_left(i)
+            if i > 0:
+                finish(i - 1)
+            fetch_right(i)
+        finish(len(pieces) - 1)

@@ -63,7 +63,8 @@ def tile_list_thickener_reagent_scores_kernel(
         tab_s = kept([P, T], U8, "tab_s")
         tab2_s = kept([P, T3], U8, "tab2_s")
         page = [kept([P, T2], F32, "page%d" % s) for s in range(SLICES)]
-        res_t = [kept([P, S], F32, "res%d" % s) for s in range(SLICES)]
+        res_b = [kept([P, PACK, S], F32, "res%d" % b) for b in range(RP)]
+        res_t = [res_b[s // PACK][:, s % PACK, :] for s in range(SLICES)]
         rake_t = [kept([P, NOUT], F32, "rake%d" % m) for m in range(MT)]
         wgs_raw = kept([P, S], F32, "wgs_raw")
         gain_t = kept([P, RP, PACK], F32, "gain_t")
@@ -71,7 +72,7 @@ def tile_list_thickener_reagent_scores_kernel(
         flow_t = kept([P, MT], F32, "flow_t")
         ident = kept([P, P], F32, "ident")
 
-        res_rows = res.rearrange("(b p t) j -> b t p j", b=RP, t=PACK)
+        res_rows = res.rearrange("(b p t) j -> b p t j", b=RP, t=PACK)
         page_rows = page0.rearrange("(b p t) n -> b t p n", b=RP, t=PACK)
 
         def load_list(name, src):
@@ -84,8 +85,9 @@ def tile_list_thickener_reagent_scores_kernel(
             rows = w1[a * PASS : (a + 1) * PASS, b * PASS : (b + 1) * PASS]
             nc.sync.dma_start(out=w_raw[a, b][:], in_=rows.rearrange("(p j) c -> p j c", j=PACK))
 
-        def load_res(s):
-            nc.sync.dma_start(out=res_t[s][:], in_=res_rows[s // PACK, s % PACK])
+        def load_res(s, count=1):
+            b, t = divmod(s, PACK)
+            nc.sync.dma_start(out=res_b[b][:, t : t + count, :], in_=res_rows[b, :, t : t + count, :])
 
         def load_page(s):
             nc.sync.dma_start(out=page[s][:], in_=page_rows[s // PACK, s % PACK])
@@ -102,19 +104,19 @@ def tile_list_thickener_reagent_scores_kernel(
         make_identity(nc, ident[:])
         nc.vector.memset(tab2_s[:].bitcast(I32), 0)
 
-        load_words(tab_w[0], tab_words[0])
-        load_list("offs", offs)
         load_w(0, 0)
+        load_list("offs", offs)
         nc.sync.dma_start(out=wgs_raw[:], in_=wgs)
+        load_words(tab_w[0], tab_words[0])
         load_w(1, 0)
         load_words(tab_w[1], tab_words[1])
-        nc.sync.dma_start(out=gain_t[:], in_=gain.rearrange("(b p t) -> p b t", b=RP, t=PACK))
         load_w(2, 0)
         load_words(tab_w[2], tab_words[2])
-        load_list("offs3", offs3)
+        nc.sync.dma_start(out=gain_t[:], in_=gain.rearrange("(b p t) -> p b t", b=RP, t=PACK))
         load_res(0)
-        load_res(1)
+        load_list("offs3", offs3)
         load_page(0)
+        load_res(1)
         load_w(0, 1)
         nc.sync.dma_start(out=gain2_t[:], in_=gain2.rearrange("(b p t) -> p b t", b=RP, t=PACK))
         load_res(2)
@@ -123,11 +125,9 @@ def tile_list_thickener_reagent_scores_kernel(
         load_res(3)
         load_page(2)
         load_w(2, 1)
-        load_res(4)
-        load_res(5)
-        load_page(4)
+        load_res(4, 3)
         load_page(3)
-        load_res(6)
+        load_page(4)
         load_res(7)
         load_page(5)
         load_page(6)
@@ -142,6 +142,9 @@ def tile_list_thickener_reagent_scores_kernel(
             nc.sync.dma_start(out=flow_t[:], in_=flow.rearrange("(m p) -> p m", p=P))
         for m in range(MT):
             nc.sync.dma_start(out=rake_t[m][:], in_=rake[m * P : (m + 1) * P, :])
+
+        warm = kept([P, 1], F32, "warm")
+        nc.scalar.activation(out=warm[:], in_=ident[:, 0:1], func=TANH)
 
         turned = bank("turned")
         for c in range(4):
@@ -167,17 +170,18 @@ def tile_list_thickener_reagent_scores_kernel(
         v_s = kept([P, S], U8, "v_s")
         w_codes, w_scales = {}, {}
 
-        def gather_v(a):
-            nc.vector.tensor_copy(v_w[a][:], tab_w[a][:].indirect(lists["offs"][:]))
+        def gather_v(a, lo=0, hi=S):
+            nc.vector.tensor_copy(v_w[a][:, lo:hi], tab_w[a][:].indirect(lists["offs"][:, lo // 16 : hi // 16]))
 
         def quantise_w(a, b):
             grouped = ring.tile([P, PACK, P, PACK], BF16, name="w_grouped", align_bytes=64)
             dst = grouped[:].rearrange("p t m j -> p m j t")
             src = w_raw[a, b][:].rearrange("p j (m t) -> p m j t", t=PACK)
-            if b == 0:
-                nc.vector.tensor_copy(out=dst, in_=src)
-            else:
-                nc.scalar.copy(out=dst, in_=src)
+            share = 0 if b == 1 else (88 if a == KP - 1 else P)
+            if share > 0:
+                nc.vector.tensor_copy(out=dst[:, :share], in_=src[:, :share])
+            if share < P:
+                nc.scalar.copy(out=dst[:, share:], in_=src[:, share:])
             w_codes[a, b] = kept([P, PASS], U32, "w_codes%d%d" % (a, b))
             w_scales[a, b] = kept([P, PASS], U8, "w_scales%d%d" % (a, b))
             nc.vector.quantize_mx(
@@ -185,43 +189,46 @@ def tile_list_thickener_reagent_scores_kernel(
                 in_=grouped[:].rearrange("p t m j -> p (t m j)"),
             )
 
-        gather_v(0)
         quantise_w(0, 0)
+        gather_v(0)
+        nc.vector.tensor_copy(v_s[:], tab_s[:].indirect(lists["offs"][:]))
         quantise_w(1, 0)
         gather_v(1)
-        nc.vector.tensor_copy(v_s[:], tab_s[:].indirect(lists["offs"][:]))
         quantise_w(2, 0)
-        gather_v(2)
+        gather_v(2, 0, S // 2)
+        gather_v(2, S // 2, S)
 
         squashed, feature = {}, {}
 
-        def first_product(s):
+        def first_product(s, lo=0, hi=S):
             b, t = divmod(s, PACK)
-            z = bank("z%d" % s)
+            z = bank("z%d_%d" % (s, lo))
             cols = slice(t * P, (t + 1) * P)
             for a in range(KP):
                 nc.tensor.matmul_mx(
-                    out=z[:], lhsT=w_codes[a, b][:, cols].bitcast(FP8X4), lhsT_scale=w_scales[a, b][:, cols],
-                    rhs=v_w[a][:].bitcast(FP8X4), rhs_scale=v_s[4 * a : P, :],
+                    out=z[:, lo:hi], lhsT=w_codes[a, b][:, cols].bitcast(FP8X4), lhsT_scale=w_scales[a, b][:, cols],
+                    rhs=v_w[a][:, lo:hi].bitcast(FP8X4), rhs_scale=v_s[4 * a : P, lo:hi],
                     start=(a == 0), stop=(a == KP - 1),
                 )
-            squashed[s] = ring.tile([P, S], F32, name="squashed", bufs=4)
-            nc.scalar.activation(out=squashed[s][:], in_=z[:], func=TANH)
+            if lo == 0:
+                squashed[s] = ring.tile([P, S], F32, name="squashed", bufs=4)
+            nc.scalar.activation(out=squashed[s][:, lo:hi], in_=z[:, lo:hi], func=TANH)
 
-        def make_feature(s):
+        def make_feature(s, lo=0, hi=S):
             b, t = divmod(s, PACK)
-            if s < SLICES - 1:
-                feature[s] = ring.tile([P, S], F32, name="feature", bufs=3)
-            else:
+            if s == SLICES - 1:
                 feature[s] = laid([P, S], F32, "feature_last", 74 * KB)
+            elif lo == 0:
+                feature[s] = ring.tile([P, S], F32, name="feature", bufs=3)
             nc.vector.scalar_tensor_tensor(
-                out=feature[s][:], in0=squashed[s][:], scalar=gain_t[:, b, t : t + 1], in1=res_t[s][:],
-                op0=MULT, op1=ADD,
+                out=feature[s][:, lo:hi], in0=squashed[s][:, lo:hi], scalar=gain_t[:, b, t : t + 1],
+                in1=res_t[s][:, lo:hi], op0=MULT, op1=ADD,
             )
 
-        def scatter(s):
+        def scatter(s, lo=0, hi=S):
             nc.vector.tensor_tensor(
-                page[s][:].indirect(lists["offs3"][:]), feature[s][:], wgs_t[s % PACK][:], MULT
+                page[s][:].indirect(lists["offs3"][:, lo // 16 : hi // 16]),
+                feature[s][:, lo:hi], wgs_t[s % PACK][:, lo:hi], MULT,
             )
 
         pairs = {}
@@ -257,12 +264,16 @@ def tile_list_thickener_reagent_scores_kernel(
                 in_=x_grouped[b, h][:].rearrange("p n t -> p (n t)"),
             )
 
-        for s in range(PACK):
+        first_product(0, 0, S // 2)
+        first_product(0, S // 2, S)
+        for s in range(1, PACK):
             first_product(s)
-        make_feature(0)
+        make_feature(0, 0, S // 2)
+        scatter(0, 0, S // 2)
+        make_feature(0, S // 2, S)
         for s in range(PACK - 1):
             make_feature(s + 1)
-            scatter(s)
+            scatter(s, S // 2 if s == 0 else 0, S)
             quantise_w(s, 1)
         for s in range(PACK, SLICES):
             first_product(s)

@@ -100,7 +100,7 @@ def tile_list_thickener_reagent_scores_kernel(
                 )
 
         nc.vector.memset(tab_s[:].bitcast(I32), 0)
-        load_scales(nc.scalar, tab_s, tab_scales, KP)
+        load_scales(nc.gpsimd, tab_s, tab_scales, KP)
         make_identity(nc, ident[:])
         nc.vector.memset(tab2_s[:].bitcast(I32), 0)
 
@@ -127,8 +127,8 @@ def tile_list_thickener_reagent_scores_kernel(
         load_w(2, 1)
         load_res(4, 3)
         load_page(3)
-        load_page(4)
         load_res(7)
+        load_page(4)
         load_page(5)
         load_page(6)
         load_page(7)
@@ -269,8 +269,8 @@ def tile_list_thickener_reagent_scores_kernel(
         for s in range(1, PACK):
             first_product(s)
         make_feature(0, 0, S // 2)
-        scatter(0, 0, S // 2)
         make_feature(0, S // 2, S)
+        scatter(0, 0, S // 2)
         for s in range(PACK - 1):
             make_feature(s + 1)
             scatter(s, S // 2 if s == 0 else 0, S)

@@ -25,9 +25,27 @@ PASS = P * PACK
 KP = K // PASS
 RP = H // PASS
 SLICES = RP * PACK
+QUADS, QUAD = 4, 32
+SCALE_ROWS = 4
+STRIPE = 16
 HALF = T2 // 2
 MT = S2 // P
+BLOCKS = S // P
+PSUM_BANKS = 8
+
+VECTOR_SHARE = 88
+
 KB = 1024
+AT_TAB_WORDS = 0
+AT_W_RAW = 24 * KB
+AT_LAST_WGS = 72 * KB
+AT_LAST_FEATURE = 74 * KB
+AT_LAST_X = 76 * KB
+AT_X_GROUPED = {(0, 0): 0, (0, 1): 4 * KB, (1, 0): 12 * KB, (1, 1): AT_LAST_X}
+AT_X_CODES = (8 * KB, 16 * KB)
+AT_X_SCALES = (AT_LAST_FEATURE + KB, 20 * KB)
+AT_PAIRS = (AT_W_RAW + 40 * KB, AT_W_RAW)
+AT_LEFT, AT_RIGHT, AT_RESULT = 32 * KB, 36 * KB, 40 * KB
 
 
 def tile_list_thickener_reagent_scores_kernel(
@@ -39,7 +57,7 @@ def tile_list_thickener_reagent_scores_kernel(
         held = ctx.enter_context(tc.tile_pool(name="held", bufs=1))
         lay = ctx.enter_context(tc.tile_pool(name="lay", bufs=1))
         ring = ctx.enter_context(tc.tile_pool(name="ring", bufs=2))
-        psum = ctx.enter_context(tc.psum_pool(name="psum", bufs=8))
+        psum = ctx.enter_context(tc.psum_pool(name="psum", bufs=PSUM_BANKS))
 
         def kept(shape, dtype, name):
             return held.tile(shape, dtype, name=name, align_bytes=64)
@@ -52,13 +70,16 @@ def tile_list_thickener_reagent_scores_kernel(
 
         lists = {}
         for name in ("offs", "offs2", "offs3", "pos1", "pos2"):
-            lists[name] = held.tile([P, S // 16], U16, name="list_" + name)
+            lists[name] = held.tile([P, S // STRIPE], U16, name="list_" + name)
 
-        tab_w = [laid([P, T], U32, "tab_w%d" % a, 8 * KB * a) for a in range(KP)]
+        def entries(name, lo, hi):
+            return lists[name][:, lo // STRIPE : hi // STRIPE]
+
+        tab_w = [laid([P, T], U32, "tab_w%d" % a, AT_TAB_WORDS + 8 * KB * a) for a in range(KP)]
         w_raw = {}
         for b in range(RP):
             for a in range(KP):
-                w_raw[a, b] = laid([P, PACK, PASS], F32, "w_raw%d%d" % (a, b), (24 + 8 * (KP * b + a)) * KB)
+                w_raw[a, b] = laid([P, PACK, PASS], F32, "w_raw%d%d" % (a, b), AT_W_RAW + 8 * KB * (KP * b + a))
         tab2_w = [kept([P, T3], U32, "tab2_w%d" % b) for b in range(RP)]
         tab_s = kept([P, T], U8, "tab_s")
         tab2_s = kept([P, T3], U8, "tab2_s")
@@ -92,11 +113,14 @@ def tile_list_thickener_reagent_scores_kernel(
         def load_page(s):
             nc.sync.dma_start(out=page[s][:], in_=page_rows[s // PACK, s % PACK])
 
+        def load_row_factor(dst, src):
+            nc.sync.dma_start(out=dst[:], in_=src.rearrange("(b p t) -> p b t", b=RP, t=PACK))
+
         def load_scales(queue, dst, src, passes):
-            for q in range(4):
+            for q in range(QUADS):
                 queue.dma_start(
-                    out=dst[32 * q : 32 * q + 4 * passes, :].bitcast(I32),
-                    in_=src[:, 4 * q : 4 * q + 4, :].bitcast(I32),
+                    out=dst[QUAD * q : QUAD * q + SCALE_ROWS * passes, :].bitcast(I32),
+                    in_=src[:, SCALE_ROWS * q : SCALE_ROWS * (q + 1), :].bitcast(I32),
                 )
 
         nc.vector.memset(tab_s[:].bitcast(I32), 0)
@@ -107,31 +131,26 @@ def tile_list_thickener_reagent_scores_kernel(
         load_w(0, 0)
         load_list("offs", offs)
         nc.sync.dma_start(out=wgs_raw[:], in_=wgs)
-        load_words(tab_w[0], tab_words[0])
-        load_w(1, 0)
-        load_words(tab_w[1], tab_words[1])
-        load_w(2, 0)
-        load_words(tab_w[2], tab_words[2])
-        nc.sync.dma_start(out=gain_t[:], in_=gain.rearrange("(b p t) -> p b t", b=RP, t=PACK))
+        for a in range(KP):
+            load_words(tab_w[a], tab_words[a])
+            if a + 1 < KP:
+                load_w(a + 1, 0)
+        load_row_factor(gain_t, gain)
         load_res(0)
         load_list("offs3", offs3)
         load_page(0)
         load_res(1)
         load_w(0, 1)
-        nc.sync.dma_start(out=gain2_t[:], in_=gain2.rearrange("(b p t) -> p b t", b=RP, t=PACK))
-        load_res(2)
-        load_page(1)
-        load_w(1, 1)
-        load_res(3)
-        load_page(2)
-        load_w(2, 1)
-        load_res(4, 3)
-        load_page(3)
-        load_res(7)
-        load_page(4)
-        load_page(5)
-        load_page(6)
-        load_page(7)
+        load_row_factor(gain2_t, gain2)
+        for s in (1, 2):
+            load_res(s + 1)
+            load_page(s)
+            load_w(s, 1)
+        load_res(PACK, PACK - 1)
+        load_page(PACK - 1)
+        load_res(SLICES - 1)
+        for s in range(PACK, SLICES):
+            load_page(s)
         load_list("offs2", offs2)
         load_scales(nc.sync, tab2_s, tab2_scales, RP)
         for b in range(RP):
@@ -143,26 +162,25 @@ def tile_list_thickener_reagent_scores_kernel(
         for m in range(MT):
             nc.sync.dma_start(out=rake_t[m][:], in_=rake[m * P : (m + 1) * P, :])
 
-        warm = kept([P, 1], F32, "warm")
-        nc.scalar.activation(out=warm[:], in_=ident[:, 0:1], func=TANH)
-
         turned = bank("turned")
-        for c in range(4):
+        for c in range(BLOCKS):
             nc.tensor.transpose(turned[:, c * P : (c + 1) * P], wgs_raw[:, c * P : (c + 1) * P], ident[:])
-        spread = kept([P, PACK, 4, 4, 32], F32, "spread")
-        for rep in range(4):
-            nc.scalar.copy(out=spread[:, :, :, rep, :], in_=turned[:].rearrange("j (c q t) -> j t c q", c=4, t=PACK))
+        spread = kept([P, PACK, BLOCKS, QUADS, QUAD], F32, "spread")
+        for quad in range(QUADS):
+            nc.scalar.copy(
+                out=spread[:, :, :, quad, :], in_=turned[:].rearrange("j (c q t) -> j t c q", c=BLOCKS, t=PACK)
+            )
         wgs_t = []
         for t in range(PACK):
             back = bank("back%d" % t)
-            for c in range(4):
+            for c in range(BLOCKS):
                 nc.tensor.transpose(
-                    back[:, c * P : (c + 1) * P], spread[:, t, c].rearrange("j r q -> j (r q)"), ident[:]
+                    back[:, c * P : (c + 1) * P], spread[:, t, c].rearrange("j quad q -> j (quad q)"), ident[:]
                 )
             if t < PACK - 1:
                 dealt = kept([P, S], F32, "wgs_t%d" % t)
             else:
-                dealt = laid([P, S], F32, "wgs_t%d" % t, 72 * KB)
+                dealt = laid([P, S], F32, "wgs_t%d" % t, AT_LAST_WGS)
             nc.scalar.copy(out=dealt[:], in_=back[:])
             wgs_t.append(dealt)
 
@@ -171,17 +189,16 @@ def tile_list_thickener_reagent_scores_kernel(
         w_codes, w_scales = {}, {}
 
         def gather_v(a, lo=0, hi=S):
-            nc.vector.tensor_copy(v_w[a][:, lo:hi], tab_w[a][:].indirect(lists["offs"][:, lo // 16 : hi // 16]))
+            nc.vector.tensor_copy(v_w[a][:, lo:hi], tab_w[a][:].indirect(entries("offs", lo, hi)))
 
-        def quantise_w(a, b):
+        def quantise_w(a, b, vector_share):
             grouped = ring.tile([P, PACK, P, PACK], BF16, name="w_grouped", align_bytes=64)
             dst = grouped[:].rearrange("p t m j -> p m j t")
             src = w_raw[a, b][:].rearrange("p j (m t) -> p m j t", t=PACK)
-            share = 0 if b == 1 else (88 if a == KP - 1 else P)
-            if share > 0:
-                nc.vector.tensor_copy(out=dst[:, :share], in_=src[:, :share])
-            if share < P:
-                nc.scalar.copy(out=dst[:, share:], in_=src[:, share:])
+            if vector_share > 0:
+                nc.vector.tensor_copy(out=dst[:, :vector_share], in_=src[:, :vector_share])
+            if vector_share < P:
+                nc.scalar.copy(out=dst[:, vector_share:], in_=src[:, vector_share:])
             w_codes[a, b] = kept([P, PASS], U32, "w_codes%d%d" % (a, b))
             w_scales[a, b] = kept([P, PASS], U8, "w_scales%d%d" % (a, b))
             nc.vector.quantize_mx(
@@ -189,12 +206,12 @@ def tile_list_thickener_reagent_scores_kernel(
                 in_=grouped[:].rearrange("p t m j -> p (t m j)"),
             )
 
-        quantise_w(0, 0)
+        quantise_w(0, 0, P)
         gather_v(0)
         nc.vector.tensor_copy(v_s[:], tab_s[:].indirect(lists["offs"][:]))
-        quantise_w(1, 0)
+        quantise_w(1, 0, P)
         gather_v(1)
-        quantise_w(2, 0)
+        quantise_w(2, 0, VECTOR_SHARE)
         gather_v(2, 0, S // 2)
         gather_v(2, S // 2, S)
 
@@ -207,17 +224,17 @@ def tile_list_thickener_reagent_scores_kernel(
             for a in range(KP):
                 nc.tensor.matmul_mx(
                     out=z[:, lo:hi], lhsT=w_codes[a, b][:, cols].bitcast(FP8X4), lhsT_scale=w_scales[a, b][:, cols],
-                    rhs=v_w[a][:, lo:hi].bitcast(FP8X4), rhs_scale=v_s[4 * a : P, lo:hi],
+                    rhs=v_w[a][:, lo:hi].bitcast(FP8X4), rhs_scale=v_s[SCALE_ROWS * a : P, lo:hi],
                     start=(a == 0), stop=(a == KP - 1),
                 )
             if lo == 0:
-                squashed[s] = ring.tile([P, S], F32, name="squashed", bufs=4)
+                squashed[s] = ring.tile([P, S], F32, name="squashed", bufs=PACK)
             nc.scalar.activation(out=squashed[s][:, lo:hi], in_=z[:, lo:hi], func=TANH)
 
         def make_feature(s, lo=0, hi=S):
             b, t = divmod(s, PACK)
             if s == SLICES - 1:
-                feature[s] = laid([P, S], F32, "feature_last", 74 * KB)
+                feature[s] = laid([P, S], F32, "feature_last", AT_LAST_FEATURE)
             elif lo == 0:
                 feature[s] = ring.tile([P, S], F32, name="feature", bufs=3)
             nc.vector.scalar_tensor_tensor(
@@ -227,22 +244,20 @@ def tile_list_thickener_reagent_scores_kernel(
 
         def scatter(s, lo=0, hi=S):
             nc.vector.tensor_tensor(
-                page[s][:].indirect(lists["offs3"][:, lo // 16 : hi // 16]),
+                page[s][:].indirect(entries("offs3", lo, hi)),
                 feature[s][:, lo:hi], wgs_t[s % PACK][:, lo:hi], MULT,
             )
 
         pairs = {}
         for h in range(2):
-            pairs[0, h] = laid([P, 2, HALF, 2], BF16, "pairs0%d" % h, (64 + 4 * h) * KB)
-            pairs[1, h] = laid([P, 2, HALF, 2], BF16, "pairs1%d" % h, (24 + 4 * h) * KB)
-        x_grouped = {
-            (0, 0): laid([P, HALF, PACK], BF16, "x_grouped00", 0),
-            (0, 1): laid([P, HALF, PACK], BF16, "x_grouped01", 4 * KB),
-            (1, 0): laid([P, HALF, PACK], BF16, "x_grouped10", 12 * KB),
-            (1, 1): laid([P, HALF, PACK], BF16, "x_grouped11", 76 * KB),
-        }
-        x_codes = [laid([P, T2], U32, "x_codes0", 8 * KB), laid([P, T2], U32, "x_codes1", 16 * KB)]
-        x_scales = [laid([P, T2], U8, "x_scales0", 75 * KB), laid([P, T2], U8, "x_scales1", 20 * KB)]
+            for b in range(RP):
+                pairs[b, h] = laid([P, 2, HALF, 2], BF16, "pairs%d%d" % (b, h), AT_PAIRS[b] + 4 * KB * h)
+        x_grouped = {}
+        for b in range(RP):
+            for h in range(2):
+                x_grouped[b, h] = laid([P, HALF, PACK], BF16, "x_grouped%d%d" % (b, h), AT_X_GROUPED[b, h])
+        x_codes = [laid([P, T2], U32, "x_codes%d" % b, AT_X_CODES[b]) for b in range(RP)]
+        x_scales = [laid([P, T2], U8, "x_scales%d" % b, AT_X_SCALES[b]) for b in range(RP)]
 
         def round_page(s, h):
             b, t = divmod(s, PACK)
@@ -271,10 +286,10 @@ def tile_list_thickener_reagent_scores_kernel(
         make_feature(0, 0, S // 2)
         make_feature(0, S // 2, S)
         scatter(0, 0, S // 2)
-        for s in range(PACK - 1):
+        for s in range(KP):
             make_feature(s + 1)
             scatter(s, S // 2 if s == 0 else 0, S)
-            quantise_w(s, 1)
+            quantise_w(s, 1, 0)
         for s in range(PACK, SLICES):
             first_product(s)
         for s in range(PACK - 1, SLICES):
@@ -294,7 +309,7 @@ def tile_list_thickener_reagent_scores_kernel(
         v2_w, v2_s = {}, {}
 
         def gather_v2(g, words_at, scales_at):
-            part = lists["offs2"][:, g * 16 : (g + 1) * 16]
+            part = entries("offs2", g * S2 // 2, (g + 1) * S2 // 2)
             v2_s[g] = laid([P, S2 // 2], U8, "v2_s%d" % g, scales_at)
             nc.vector.tensor_copy(v2_s[g][:], tab2_s[:].indirect(part))
             for b in range(RP):
@@ -303,46 +318,47 @@ def tile_list_thickener_reagent_scores_kernel(
 
         for h in range(2):
             quantise_x(0, h)
-        gather_v2(0, 72 * KB, 74 * KB)
+        gather_v2(0, AT_LAST_WGS, AT_LAST_FEATURE)
         for h in range(2):
             quantise_x(1, h)
-        gather_v2(1, 76 * KB, 78 * KB)
+        gather_v2(1, AT_LAST_X, AT_LAST_X + RP * KB)
 
         scores = []
         for m in range(MT):
-            g, mm = divmod(m, 2)
-            cols = slice(mm * P, (mm + 1) * P)
-            e = kept([P, T2], F32, "scores%d" % m)
+            g, within = divmod(m, MT // 2)
+            cols = slice(within * P, (within + 1) * P)
+            row_tile = kept([P, T2], F32, "scores%d" % m)
             for h in range(2):
-                ncols = slice(h * HALF, (h + 1) * HALF)
+                slots = slice(h * HALF, (h + 1) * HALF)
                 acc = bank("acc%d%d" % (m, h))
                 for b in range(RP):
                     nc.tensor.matmul_mx(
-                        out=acc[:], lhsT=v2_w[b, g][:, cols].bitcast(FP8X4), lhsT_scale=v2_s[g][4 * b : P, cols],
-                        rhs=x_codes[b][:, ncols].bitcast(FP8X4), rhs_scale=x_scales[b][:, ncols],
+                        out=acc[:], lhsT=v2_w[b, g][:, cols].bitcast(FP8X4),
+                        lhsT_scale=v2_s[g][SCALE_ROWS * b : P, cols],
+                        rhs=x_codes[b][:, slots].bitcast(FP8X4), rhs_scale=x_scales[b][:, slots],
                         start=(b == 0), stop=(b == RP - 1),
                     )
-                nc.scalar.copy(out=e[:, ncols], in_=acc[:])
-            scores.append(e)
+                nc.scalar.copy(out=row_tile[:, slots], in_=acc[:])
+            scores.append(row_tile)
 
         pieces = [(m, 0, NOUT) for m in range(MT - 1)] + [(MT - 1, 0, NOUT // 2), (MT - 1, NOUT // 2, NOUT)]
         left, right = {}, {}
 
         def fetch_left(i):
             m, lo, hi = pieces[i]
-            left[i] = laid([P, hi - lo], F32, "left%d" % i, (32 + 2 * (i % 2)) * KB)
+            left[i] = laid([P, hi - lo], F32, "left%d" % i, AT_LEFT + 2 * KB * (i % 2))
             nc.vector.tensor_tensor(
-                left[i][:], scores[m][:].indirect(lists["pos1"][:, lo // 16 : hi // 16]), rake_t[m][:, lo:hi], ADD
+                left[i][:], scores[m][:].indirect(entries("pos1", lo, hi)), rake_t[m][:, lo:hi], ADD
             )
 
         def fetch_right(i):
             m, lo, hi = pieces[i]
-            right[i] = laid([P, hi - lo], F32, "right%d" % i, (36 + 2 * (i % 2)) * KB)
-            nc.vector.tensor_copy(right[i][:], scores[m][:].indirect(lists["pos2"][:, lo // 16 : hi // 16]))
+            right[i] = laid([P, hi - lo], F32, "right%d" % i, AT_RIGHT + 2 * KB * (i % 2))
+            nc.vector.tensor_copy(right[i][:], scores[m][:].indirect(entries("pos2", lo, hi)))
 
         def finish(i):
             m, lo, hi = pieces[i]
-            result = laid([P, hi - lo], F32, "result%d" % i, (40 + 2 * (i % 3)) * KB)
+            result = laid([P, hi - lo], F32, "result%d" % i, AT_RESULT + 2 * KB * (i % 3))
             nc.vector.scalar_tensor_tensor(
                 out=result[:], in0=right[i][:], scalar=flow_t[:, m : m + 1], in1=left[i][:], op0=MULT, op1=MAX
             )

from contextlib import ExitStack

import concourse.mybir as mybir
from concourse.masks import make_identity

K, T, S, H, S2, T3, T2, NOUT = 1536, 2048, 512, 1024, 512, 2048, 1024, 512
FLOPS = 2 * K * H * S + 2 * H * S2 * T2

F32 = mybir.dt.float32
BF16 = mybir.dt.bfloat16
I32 = mybir.dt.int32
U32 = mybir.dt.uint32
U16 = mybir.dt.uint16
U8 = mybir.dt.uint8
FP8X4 = mybir.dt.float8_e4m3fn_x4
MULT = mybir.AluOpType.mult
ADD = mybir.AluOpType.add
MAX = mybir.AluOpType.max
COPY = mybir.ActivationFunctionType.Copy
TANH = mybir.ActivationFunctionType.Tanh

P = 128
PACK = 4
PASS = P * PACK
KP = K // PASS
RP = H // PASS
SLICES = RP * PACK
QUADS, QUAD = 4, 32
SCALE_ROWS = 4
STRIPE = 16
HALF = T2 // 2
MT = S2 // P
BLOCKS = S // P
PSUM_BANKS = 8

VECTOR_SHARE = 88

KB = 1024
AT_TAB_WORDS = 0
AT_W_RAW = 24 * KB
AT_LAST_WGS = 72 * KB
AT_LAST_FEATURE = 74 * KB
AT_LAST_X = 76 * KB
AT_X_GROUPED = {(0, 0): 0, (0, 1): 4 * KB, (1, 0): 12 * KB, (1, 1): AT_LAST_X}
AT_X_CODES = (8 * KB, 16 * KB)
AT_X_SCALES = (AT_LAST_FEATURE + KB, 20 * KB)
AT_PAIRS = (AT_W_RAW + 40 * KB, AT_W_RAW)
AT_LEFT, AT_RIGHT, AT_RESULT = 32 * KB, 36 * KB, 40 * KB


def tile_list_thickener_reagent_scores_kernel(
    tc, tab_words, tab_scales, tab2_words, tab2_scales, offs, offs2, offs3, pos1, pos2,
    w1, gain, res, wgs, page0, gain2, rake, flow, out,
):
    nc = tc.nc
    with ExitStack() as ctx:
        held = ctx.enter_context(tc.tile_pool(name="held", bufs=1))
        lay = ctx.enter_context(tc.tile_pool(name="lay", bufs=1))
        ring = ctx.enter_context(tc.tile_pool(name="ring", bufs=2))
        psum = ctx.enter_context(tc.psum_pool(name="psum", bufs=PSUM_BANKS))

        def kept(shape, dtype, name):
            return held.tile(shape, dtype, name=name, align_bytes=64)

        def laid(shape, dtype, name, at):
            return lay.tile(shape, dtype, name=name, align_bytes=64, offset=at)

        def bank(name):
            return psum.tile([P, PASS], F32, name=name, tag="bank")

        lists = {}
        for name in ("offs", "offs2", "offs3", "pos1", "pos2"):
            lists[name] = held.tile([P, S // STRIPE], U16, name="list_" + name)

        def entries(name, lo, hi):
            return lists[name][:, lo // STRIPE : hi // STRIPE]

        tab_w = [laid([P, T], U32, "tab_w%d" % a, AT_TAB_WORDS + 8 * KB * a) for a in range(KP)]
        w_raw = {}
        for b in range(RP):
            for a in range(KP):
                w_raw[a, b] = laid([P, PACK, PASS], F32, "w_raw%d%d" % (a, b), AT_W_RAW + 8 * KB * (KP * b + a))
        tab2_w = [kept([P, T3], U32, "tab2_w%d" % b) for b in range(RP)]
        tab_s = kept([P, T], U8, "tab_s")
        tab2_s = kept([P, T3], U8, "tab2_s")
        page = [kept([P, T2], F32, "page%d" % s) for s in range(SLICES)]
        res_b = [kept([P, PACK, S], F32, "res%d" % b) for b in range(RP)]
        res_t = [res_b[s // PACK][:, s % PACK, :] for s in range(SLICES)]
        rake_t = [kept([P, NOUT], F32, "rake%d" % m) for m in range(MT)]
        wgs_raw = kept([P, S], F32, "wgs_raw")
        gain_t = kept([P, RP, PACK], F32, "gain_t")
        gain2_t = kept([P, RP, PACK], F32, "gain2_t")
        flow_t = kept([P, MT], F32, "flow_t")
        ident = kept([P, P], F32, "ident")

        res_rows = res.rearrange("(b p t) j -> b p t j", b=RP, t=PACK)
        page_rows = page0.rearrange("(b p t) n -> b t p n", b=RP, t=PACK)

        def load_list(name, src):
            nc.sync.dma_start(lists[name][:], src)

        def load_words(dst, src):
            nc.sync.dma_start(out=dst[:].bitcast(I32), in_=src.rearrange("p n t -> p (n t)").bitcast(I32))

        def load_w(a, b):
            rows = w1[a * PASS : (a + 1) * PASS, b * PASS : (b + 1) * PASS]
            nc.sync.dma_start(out=w_raw[a, b][:], in_=rows.rearrange("(p j) c -> p j c", j=PACK))

        def load_res(s, count=1):
            b, t = divmod(s, PACK)
            nc.sync.dma_start(out=res_b[b][:, t : t + count, :], in_=res_rows[b, :, t : t + count, :])

        def load_page(s):
            nc.sync.dma_start(out=page[s][:], in_=page_rows[s // PACK, s % PACK])

        def load_row_factor(dst, src):
            nc.sync.dma_start(out=dst[:], in_=src.rearrange("(b p t) -> p b t", b=RP, t=PACK))

        def load_scales(queue, dst, src, passes):
            for q in range(QUADS):
                queue.dma_start(
                    out=dst[QUAD * q : QUAD * q + SCALE_ROWS * passes, :].bitcast(I32),
                    in_=src[:, SCALE_ROWS * q : SCALE_ROWS * (q + 1), :].bitcast(I32),
                )

        nc.vector.memset(tab_s[:].bitcast(I32), 0)
        load_scales(nc.gpsimd, tab_s, tab_scales, KP)
        make_identity(nc, ident[:])
        nc.vector.memset(tab2_s[:].bitcast(I32), 0)

        load_w(0, 0)
        load_list("offs", offs)
        nc.sync.dma_start(out=wgs_raw[:], in_=wgs)
        for a in range(KP):
            load_words(tab_w[a], tab_words[a])
            if a + 1 < KP:
                load_w(a + 1, 0)
        load_row_factor(gain_t, gain)
        load_res(0)
        load_list("offs3", offs3)
        load_page(0)
        load_res(1)
        load_w(0, 1)
        load_row_factor(gain2_t, gain2)
        for s in (1, 2):
            load_res(s + 1)
            load_page(s)
            load_w(s, 1)
        load_res(PACK, PACK - 1)
        load_page(PACK - 1)
        load_res(SLICES - 1)
        for s in range(PACK, SLICES):
            load_page(s)
        load_list("offs2", offs2)
        load_scales(nc.sync, tab2_s, tab2_scales, RP)
        for b in range(RP):
            load_words(tab2_w[b], tab2_words[b])
        load_list("pos1", pos1)
        load_list("pos2", pos2)
        with nc.allow_non_contiguous_dma(reason="one factor a partition"):
            nc.sync.dma_start(out=flow_t[:], in_=flow.rearrange("(m p) -> p m", p=P))
        for m in range(MT):
            nc.sync.dma_start(out=rake_t[m][:], in_=rake[m * P : (m + 1) * P, :])

        turned = bank("turned")
        for c in range(BLOCKS):
            nc.tensor.transpose(turned[:, c * P : (c + 1) * P], wgs_raw[:, c * P : (c + 1) * P], ident[:])
        spread = kept([P, PACK, BLOCKS, QUADS, QUAD], F32, "spread")
        for quad in range(QUADS):
            nc.scalar.copy(
                out=spread[:, :, :, quad, :], in_=turned[:].rearrange("j (c q t) -> j t c q", c=BLOCKS, t=PACK)
            )
        wgs_t = []
        for t in range(PACK):
            back = bank("back%d" % t)
            for c in range(BLOCKS):
                nc.tensor.transpose(
                    back[:, c * P : (c + 1) * P], spread[:, t, c].rearrange("j quad q -> j (quad q)"), ident[:]
                )
            if t < PACK - 1:
                dealt = kept([P, S], F32, "wgs_t%d" % t)
            else:
                dealt = laid([P, S], F32, "wgs_t%d" % t, AT_LAST_WGS)
            nc.scalar.copy(out=dealt[:], in_=back[:])
            wgs_t.append(dealt)

        v_w = [kept([P, S], U32, "v_w%d" % a) for a in range(KP)]
        v_s = kept([P, S], U8, "v_s")
        w_codes, w_scales = {}, {}

        def gather_v(a, lo=0, hi=S):
            nc.vector.tensor_copy(v_w[a][:, lo:hi], tab_w[a][:].indirect(entries("offs", lo, hi)))

        def quantise_w(a, b, vector_share):
            grouped = ring.tile([P, PACK, P, PACK], BF16, name="w_grouped", align_bytes=64)
            dst = grouped[:].rearrange("p t m j -> p m j t")
            src = w_raw[a, b][:].rearrange("p j (m t) -> p m j t", t=PACK)
            if vector_share > 0:
                nc.vector.tensor_copy(out=dst[:, :vector_share], in_=src[:, :vector_share])
            if vector_share < P:
                nc.scalar.copy(out=dst[:, vector_share:], in_=src[:, vector_share:])
            w_codes[a, b] = kept([P, PASS], U32, "w_codes%d%d" % (a, b))
            w_scales[a, b] = kept([P, PASS], U8, "w_scales%d%d" % (a, b))
            nc.vector.quantize_mx(
                out=w_codes[a, b][:].bitcast(FP8X4), scales=w_scales[a, b][:],
                in_=grouped[:].rearrange("p t m j -> p (t m j)"),
            )

        quantise_w(0, 0, P)
        gather_v(0)
        nc.vector.tensor_copy(v_s[:], tab_s[:].indirect(lists["offs"][:]))
        quantise_w(1, 0, P)
        gather_v(1)
        quantise_w(2, 0, VECTOR_SHARE)
        gather_v(2, 0, S // 2)
        gather_v(2, S // 2, S)

        squashed, feature = {}, {}

        def first_product(s, lo=0, hi=S):
            b, t = divmod(s, PACK)
            z = bank("z%d_%d" % (s, lo))
            cols = slice(t * P, (t + 1) * P)
            for a in range(KP):
                nc.tensor.matmul_mx(
                    out=z[:, lo:hi], lhsT=w_codes[a, b][:, cols].bitcast(FP8X4), lhsT_scale=w_scales[a, b][:, cols],
                    rhs=v_w[a][:, lo:hi].bitcast(FP8X4), rhs_scale=v_s[SCALE_ROWS * a : P, lo:hi],
                    start=(a == 0), stop=(a == KP - 1),
                )
            if lo == 0:
                squashed[s] = ring.tile([P, S], F32, name="squashed", bufs=PACK)
            nc.scalar.activation(out=squashed[s][:, lo:hi], in_=z[:, lo:hi], func=TANH)

        def make_feature(s, lo=0, hi=S):
            b, t = divmod(s, PACK)
            if s == SLICES - 1:
                feature[s] = laid([P, S], F32, "feature_last", AT_LAST_FEATURE)
            elif lo == 0:
                feature[s] = ring.tile([P, S], F32, name="feature", bufs=3)
            nc.vector.scalar_tensor_tensor(
                out=feature[s][:, lo:hi], in0=squashed[s][:, lo:hi], scalar=gain_t[:, b, t : t + 1],
                in1=res_t[s][:, lo:hi], op0=MULT, op1=ADD,
            )

        def scatter(s, lo=0, hi=S):
            nc.vector.tensor_tensor(
                page[s][:].indirect(entries("offs3", lo, hi)),
                feature[s][:, lo:hi], wgs_t[s % PACK][:, lo:hi], MULT,
            )

        pairs = {}
        for h in range(2):
            for b in range(RP):
                pairs[b, h] = laid([P, 2, HALF, 2], BF16, "pairs%d%d" % (b, h), AT_PAIRS[b] + 4 * KB * h)
        x_grouped = {}
        for b in range(RP):
            for h in range(2):
                x_grouped[b, h] = laid([P, HALF, PACK], BF16, "x_grouped%d%d" % (b, h), AT_X_GROUPED[b, h])
        x_codes = [laid([P, T2], U32, "x_codes%d" % b, AT_X_CODES[b]) for b in range(RP)]
        x_scales = [laid([P, T2], U8, "x_scales%d" % b, AT_X_SCALES[b]) for b in range(RP)]

        def round_page(s, h):
            b, t = divmod(s, PACK)
            nc.scalar.activation(
                out=pairs[b, h][:, t // 2, :, t % 2], in_=page[s][:, h * HALF : (h + 1) * HALF],
                func=COPY, scale=gain2_t[:, b, t : t + 1],
            )

        def weave_x(b, h):
            nc.scalar.copy(
                out=x_grouped[b, h][:].bitcast(U32),
                in_=pairs[b, h][:].bitcast(U32).rearrange("p u n one -> p n (u one)"),
            )

        def quantise_x(b, h):
            cols = slice(h * HALF, (h + 1) * HALF)
            nc.vector.quantize_mx(
                out=x_codes[b][:, cols].bitcast(FP8X4), scales=x_scales[b][:, cols],
                in_=x_grouped[b, h][:].rearrange("p n t -> p (n t)"),
            )

        first_product(0, 0, S // 2)
        first_product(0, S // 2, S)
        for s in range(1, PACK):
            first_product(s)
        make_feature(0, 0, S // 2)
        make_feature(0, S // 2, S)
        scatter(0, 0, S // 2)
        for s in range(KP):
            make_feature(s + 1)
            scatter(s, S // 2 if s == 0 else 0, S)
            quantise_w(s, 1, 0)
        for s in range(PACK, SLICES):
            first_product(s)
        for s in range(PACK - 1, SLICES):
            if s + 1 < SLICES:
                make_feature(s + 1)
            scatter(s)
        for s in range(SLICES - 1):
            for h in range(2):
                round_page(s, h)
            if s == PACK - 1:
                for h in range(2):
                    weave_x(0, h)
        for h in range(2):
            round_page(SLICES - 1, h)
            weave_x(1, h)

        v2_w, v2_s = {}, {}

        def gather_v2(g, words_at, scales_at):
            part = entries("offs2", g * S2 // 2, (g + 1) * S2 // 2)
            v2_s[g] = laid([P, S2 // 2], U8, "v2_s%d" % g, scales_at)
            nc.vector.tensor_copy(v2_s[g][:], tab2_s[:].indirect(part))
            for b in range(RP):
                v2_w[b, g] = laid([P, S2 // 2], U32, "v2_w%d%d" % (b, g), words_at + b * KB)
                nc.vector.tensor_copy(v2_w[b, g][:], tab2_w[b][:].indirect(part))

        for h in range(2):
            quantise_x(0, h)
        gather_v2(0, AT_LAST_WGS, AT_LAST_FEATURE)
        for h in range(2):
            quantise_x(1, h)
        gather_v2(1, AT_LAST_X, AT_LAST_X + RP * KB)

        scores = []
        for m in range(MT):
            g, within = divmod(m, MT // 2)
            cols = slice(within * P, (within + 1) * P)
            row_tile = kept([P, T2], F32, "scores%d" % m)
            for h in range(2):
                slots = slice(h * HALF, (h + 1) * HALF)
                acc = bank("acc%d%d" % (m, h))
                for b in range(RP):
                    nc.tensor.matmul_mx(
                        out=acc[:], lhsT=v2_w[b, g][:, cols].bitcast(FP8X4),
                        lhsT_scale=v2_s[g][SCALE_ROWS * b : P, cols],
                        rhs=x_codes[b][:, slots].bitcast(FP8X4), rhs_scale=x_scales[b][:, slots],
                        start=(b == 0), stop=(b == RP - 1),
                    )
                nc.scalar.copy(out=row_tile[:, slots], in_=acc[:])
            scores.append(row_tile)

        pieces = [(m, 0, NOUT) for m in range(MT - 1)] + [(MT - 1, 0, NOUT // 2), (MT - 1, NOUT // 2, NOUT)]
        left, right = {}, {}

        def fetch_left(i):
            m, lo, hi = pieces[i]
            left[i] = laid([P, hi - lo], F32, "left%d" % i, AT_LEFT + 2 * KB * (i % 2))
            nc.vector.tensor_tensor(
                left[i][:], scores[m][:].indirect(entries("pos1", lo, hi)), rake_t[m][:, lo:hi], ADD
            )

        def fetch_right(i):
            m, lo, hi = pieces[i]
            right[i] = laid([P, hi - lo], F32, "right%d" % i, AT_RIGHT + 2 * KB * (i % 2))
            nc.vector.tensor_copy(right[i][:], scores[m][:].indirect(entries("pos2", lo, hi)))

        def finish(i):
            m, lo, hi = pieces[i]
            result = laid([P, hi - lo], F32, "result%d" % i, AT_RESULT + 2 * KB * (i % 3))
            nc.vector.scalar_tensor_tensor(
                out=result[:], in0=right[i][:], scalar=flow_t[:, m : m + 1], in1=left[i][:], op0=MULT, op1=MAX
            )
            nc.sync.dma_start(out=out[m * P : (m + 1) * P, lo:hi], in_=result[:])

        for i in range(len(pieces)):
            fetch_left(i)
            if i > 0:
                finish(i - 1)
            fetch_right(i)
        finish(len(pieces) - 1)
